import numpy as np
CORES = [129,145,193,257,273,321,385,401,449]
N = 9
R, T = 2048, 1024
CAPP = 256
def entries(a): return a.T.reshape(-1)
def pack(v, P): return np.ascontiguousarray(np.asarray(v, np.int32).reshape(-1, P).T)
def lists(rng, how):
    I = rng.integers(0, N * R, (N, T))
    O = np.stack([rng.permutation(np.repeat(np.arange(N), CAPP))[:T] for r in range(N)])
    if how == "full": O = np.stack([rng.permutation(np.repeat(rng.permutation(N)[:T // CAPP], CAPP)) for r in range(N)])
    I = R * O + rng.integers(0, R, (N, T))
    if how == "alike": I = R * O + rng.integers(0, R, (N, 1))
    if how == "edge": I = R * O + np.where(rng.random((N, T)) < 0.5, 0, R - 1)
    if how == "sorted": I = np.sort(I, axis=1)
    return {"idx": np.stack([pack(I[r], 16) for r in range(N)])}
def setup_inputs(rng):
    return dict({"x": rng.standard_normal((N, 128, T), dtype=np.float32), "tab": rng.standard_normal((N, 128, R), dtype=np.float32)}, **lists(rng, "uniform"))
def setup_inputs_alike(rng):
    d = setup_inputs(rng); d.update(lists(rng, "alike"))
    for k in ("x", "tab"): d[k] = (d[k].astype(np.float32) * 1024.0).astype(d[k].dtype)
    return d
def setup_inputs_edge(rng):
    d = setup_inputs(rng); d.update(lists(rng, "edge"))
    for k in ("x", "tab"): d[k] = (d[k].astype(np.float32) * (1 / 1024.0)).astype(d[k].dtype)
    return d
def setup_inputs_full(rng):
    d = setup_inputs(rng); d.update(lists(rng, "full"))
    return d
def setup_inputs_sorted(rng):
    d = setup_inputs(rng); d.update(lists(rng, "sorted"))
    return d
def check_inputs(x):
    bad = []
    if x["idx"].min() < 0 or x["idx"].max() >= N * R: bad.append("idx out of range")
    if max(int(np.bincount(entries(a) // R, minlength=N).max()) for a in x["idx"]) > CAPP: bad.append("more than CAPP entries of a list point into one rank's part")
    return bad
def reference(x, tab, idx):
    A = np.concatenate(list(tab), axis=1).astype(np.float64)
    return {"y": np.stack([x[r].astype(np.float64) + A[:, entries(idx[r])] for r in range(N)]).astype(np.float32)}

@@ -1,0 +1,360 @@
+from concourse.bass import DstId, RemoteDMATransfer
+from concourse.mybir import AluOpType, ActivationFunctionType
+
+NR = 9
+RC = 2048
+CAP = 256
+NS = NR - 1
+LAND = NS * CAP
+
+SCRATCH = {
+    "big": ("sbuf", [128, LAND + RC], "float32"),
+    "resp": ("sbuf", [128, 4 * CAP], "float32"),
+    "xs": ("sbuf", [128, 1024], "float32"),
+    "idxk": ("sbuf", [128, 8], "int32"),
+    "own": ("sbuf", [128, 8], "int32"),
+    "loci": ("sbuf", [128, 8], "int32"),
+    "locf": ("sbuf", [128, 8], "float32"),
+    "oh": ("sbuf", [128, 64], "bfloat16"),
+    "ch": ("sbuf", [128, 64], "bfloat16"),
+    "zc": ("sbuf", [128, 64], "float32"),
+    "zm": ("sbuf", [128, 64], "bfloat16"),
+    "c3": ("sbuf", [128, 64], "bfloat16"),
+    "ones": ("sbuf", [128, 128], "bfloat16"),
+    "km": ("sbuf", [128, 128], "float32"),
+    "ngt": ("sbuf", [128, 128], "bfloat16"),
+    "iq": ("sbuf", [128, 128], "float32"),
+    "iu": ("sbuf", [128, 128], "float32"),
+    "iqh": ("sbuf", [128, 128], "float16"),
+    "iuh": ("sbuf", [128, 128], "float16"),
+    "t1": ("sbuf", [128, 64], "float32"),
+    "t32": ("sbuf", [128, 32], "float32"),
+    "t16": ("sbuf", [128, 16], "float32"),
+    "pos1": ("sbuf", [128, 8], "float32"),
+    "u1": ("sbuf", [128, 8], "float32"),
+    "u16": ("sbuf", [128, 8], "float32"),
+    "am": ("sbuf", [128, 1024], "float16"),
+    "bm": ("sbuf", [128, 1024], "float16"),
+    "reqw": ("sbuf", [128, 128], "uint16"),
+    "rp": ("sbuf", [128, 128], "int32"),
+    "rp2": ("sbuf", [128, 128], "int32"),
+    "rep2": ("sbuf", [128, 128], "float32"),
+    "bmi": ("sbuf", [128, 8], "int32"),
+    "bm2i": ("sbuf", [128, 8], "int32"),
+    "bm2": ("sbuf", [128, 8], "float32"),
+    "ohme": ("sbuf", [128, 8], "float32"),
+    "l2": ("sbuf", [128, 8], "float32"),
+    "l3": ("sbuf", [128, 8], "float32"),
+    "pf": ("sbuf", [128, 8], "float32"),
+    "rbig": ("sbuf", [128, 64], "float32"),
+    "posw": ("sbuf", [128, 64], "uint16"),
+    "sp": ("psum", [128, 512], "float32"),
+    "rqp": ("psum", [128, 512], "float32"),
+    "pwp": ("psum", [128, 512], "float32"),
+}
+for _r in range(NR):
+    SCRATCH["rq%d" % _r] = ("sbuf", [128, 16], "uint16")
+
+SEMAPHORES = (["il", "tl0", "tl1", "tl2", "tl3", "xl", "vs", "ps", "gs", "rdy", "tarr", "tsent", "sent", "arr", "rsp",
+               "st", "gd0", "gd1", "gd2", "gd3", "fin0", "fin1", "fin2", "fin3"] + ["rq%d" % _r for _r in range(NR)])
+
+_PLAN = {}
+
+
+def _bits(mask):
+    return [e for e in range(16) if (mask >> e) & 1]
+
+
+def _plan(T, topo):
+    if "p" in _PLAN:
+        return _PLAN["p"]
+    R = list(T.cores)
+    n = len(R)
+    allc = range(4 * topo.CORES_PER_HOST)
+    place = lambda c: (topo.host(c), topo.chip(c))
+    bychip = {}
+    for c in allc:
+        bychip.setdefault(place(c), []).append(c)
+    rank_hosts = set(topo.host(c) for c in R)
+    H = [[c for c in bychip[place(R[o])] if topo.die(c) != topo.die(R[o])][0] for o in range(n)]
+    rackof = lambda c: topo.rack(topo.host(c))
+    diag = [(r, o) for r in range(n) for o in range(n) if r != o and not topo.may_write(R[o], R[r])]
+    groups = {}
+    for (r, o) in diag:
+        zs = [h for h in range(4) if h not in rank_hosts
+              and topo.may_write(R[r], bychip[(h, topo.chip(R[r]))][0]) and topo.may_write(R[o], bychip[(h, topo.chip(R[o]))][0])]
+        z = zs[0]
+        far = r if rackof(R[r]) != topo.rack(z) else o
+        groups.setdefault((z, topo.chip(R[far])), []).append((0 if far == r else 1, r, o))
+    relay = {}
+    for key, prs in groups.items():
+        cs = bychip[key]
+        d0 = [c for c in cs if topo.die(c) == topo.die(cs[0])]
+        d1 = [c for c in cs if topo.die(c) != topo.die(cs[0])]
+        order = []
+        for i in list(range(0, len(d0), 2)) + list(range(1, len(d0), 2)):
+            order += [d0[i], d1[i]]
+        for i, (_, r, o) in enumerate(sorted(prs)):
+            relay[(r, o)] = order[i]
+    server, jobs = {}, {}
+    for o in range(n):
+        rs = sorted([r for r in range(n) if r != o], key=lambda r: (r - o) % n)
+        nxt = {r: relay.get((r, o), R[r]) for r in rs}
+        cab = {r: rackof(nxt[r]) != rackof(R[o]) for r in rs}
+        best = None
+        for m in range(1 << len(rs)):
+            a = [rs[i] for i in range(len(rs)) if (m >> i) & 1]
+            if len(a) != len(rs) // 2:
+                continue
+            ca = sum(1 for r in a if cab[r])
+            key = (max(ca, sum(cab.values()) - ca), -sum(1 for r in a if (r, o) in relay), m)
+            if best is None or key < best[0]:
+                best = (key, a)
+        a = best[1]
+        b = [r for r in rs if r not in a]
+        for srv, mine, lead in ((R[o], a, 1), (H[o], b, 0)):
+            dg = [r for r in mine if (r, o) in relay]
+            di = [r for r in mine if (r, o) not in relay]
+            order = di[:lead] + dg + di[lead:]
+            jobs[srv] = [(r, o) for r in order]
+            for i, r in enumerate(order):
+                server[(r, o)] = (srv, i)
+    reqorder = {}
+    for r in range(n):
+        reqorder[r] = sorted([o for o in range(n) if o != r], key=lambda o: (0 if (r, o) in relay else 1, server[(r, o)][1], (o - r) % n))
+    rel_of = {}
+    for pr, c in relay.items():
+        rel_of[c] = pr
+    p = {"R": R, "H": H, "relay": relay, "server": server, "jobs": jobs, "reqorder": reqorder, "rel_of": rel_of}
+    _PLAN["p"] = p
+    return p
+
+
+def _slot(r, o):
+    return (o - r - 1) % NR
+
+
+def _send(g, core, T, topo, dst, out_ap, in_ap, rsem, lsem, mask=None):
+    rid, pid = topo.addr(dst, core)
+    m = topo.mask(core, dst) if mask is None else mask
+    g.remote_dma(out_ap, in_ap, rsem, lsem, pid, rid, m)
+    return len(_bits(m))
+
+
+def _serve(g, core, T, topo, P, tabwait):
+    jobs = P["jobs"][core]
+    for i, (r, o) in enumerate(jobs):
+        e = g.vector if i % 2 == 0 else g.scalar
+        if i < 2:
+            tabwait(e)
+        inc = len(_bits(topo.mask(P["relay"][(r, o)], core))) if (r, o) in P["relay"] else 2
+        e.wait_ge(T.sem["rq%d" % r], inc)
+        src = T.big[:, LAND:LAND + RC].indirect(T["rq%d" % r][:, :])
+        out = T.resp[:, CAP * i:CAP * (i + 1)]
+        if i % 2 == 0:
+            ins = g.vector.tensor_copy(out, src)
+        else:
+            ins = g.scalar.activation(out, src, ActivationFunctionType.Copy)
+        ins.then_inc(T.sem["gd%d" % i], 1)
+    sent = 0
+    for i, (r, o) in enumerate(jobs):
+        g.wait_ge(T.sem["gd%d" % i], 1)
+        src = T.resp[:, CAP * i:CAP * (i + 1)]
+        if (r, o) in P["relay"]:
+            sent += _send(g, core, T, topo, P["relay"][(r, o)], T.big[:, 0:CAP], src, T.sem.rsp, T.sem.sent)
+        else:
+            s = _slot(r, o)
+            sent += _send(g, core, T, topo, P["R"][r], T.big[:, CAP * s:CAP * (s + 1)], src, T.sem.arr, T.sem.sent)
+    return sent
+
+
+def _relay(g, core, T, topo, P):
+    r, o = P["rel_of"][core]
+    srv = P["server"][(r, o)][0]
+    buf = T["rq%d" % r]
+    g.wait_ge(T.sem["rq%d" % r], 2)
+    sent = _send(g, core, T, topo, srv, buf[:, :], buf[:, :], T.sem["rq%d" % r], T.sem.sent)
+    g.wait_ge(T.sem.rsp, len(_bits(topo.mask(srv, core))))
+    s = _slot(r, o)
+    sent += _send(g, core, T, topo, P["R"][r], T.big[:, CAP * s:CAP * (s + 1)], T.big[:, 0:CAP], T.sem.arr, T.sem.sent)
+    g.wait_ge(T.sem.sent, sent)
+
+
+def _helper(g, core, T, topo, P, owner):
+    up = len(_bits(_upmask(topo, P, owner)))
+
+    def tabwait(e):
+        e.wait_ge(T.sem.tarr, 2 * up)
+    sent = _serve(g, core, T, topo, P, tabwait)
+    g.wait_ge(T.sem.sent, sent)
+
+
+def _upmask(topo, P, o):
+    other = P["R"][(o + 1) % NR]
+    return topo.mask(P["R"][o], P["H"][o]) & ~topo.mask(P["R"][o], other)
+
+
+def _rank(g, core, T, topo, P):
+    A = AluOpType
+    v, pe, sc, sy = g.vector, g.tensor, g.scalar, g.sync
+    S = T.sem
+    me = T.rank_of(core)
+    c = {"v": 0, "p": 0, "g": 0}
+
+    def V(ins):
+        ins.then_inc(S.vs, 1)
+        c["v"] += 1
+
+    def vw():
+        v.wait_ge(S.vs, c["v"])
+
+    def G(ins):
+        ins.then_inc(S.gs, 1)
+        c["g"] += 1
+
+    def PEI(ins):
+        ins.then_inc(S.ps, 1)
+        c["p"] += 1
+
+    sy.dma_start(T.idxk[:, :], T.idx[:, :]).then_inc(S.il, 16)
+    for i in range(4):
+        q = sy if i % 2 == 0 else sc
+        q.dma_start(T.big[:, LAND + 512 * i:LAND + 512 * (i + 1)], T.tab[:, 512 * i:512 * (i + 1)]).then_inc(S["tl%d" % i], 16)
+
+    G(g.iota(T.c3[:, :], [[2, 8], [0, 8]], 0, 0, allow_small_or_imprecise_dtypes=True))
+    G(g.iota(T.zc[:, :], [[0, 8], [1, 8]], 0, 0, allow_small_or_imprecise_dtypes=True))
+    G(g.iota(T.km[:, :], [[-1, 128]], 0, 1, allow_small_or_imprecise_dtypes=True))
+    G(g.iota(T.iq[:, :], [[0, 8], [1, 16]], 1, 0, allow_small_or_imprecise_dtypes=True))
+    G(g.iota(T.iu[:, :], [[16, 128]], 0, 0, allow_small_or_imprecise_dtypes=True))
+    G(g.iota(T.rp[:, :], [[0, 8], [-8, 16]], 0, 1))
+    G(g.iota(T.bmi[:, :], [[-1, 8]], 8, 1))
+    V(v.memset(T.ones[:, :], 1.0))
+    pe.wait_ge(S.gs, 1)
+    pe.wait_ge(S.vs, 1)
+    pe.matmul(T.sp[:, 0:64], T.ones[:, :], T.c3[:, :], True, False)
+    v.wait_ge(S.gs, 2)
+    V(v.tensor_scalar(T.zm[:, :], T.zc[:, :], 1.0, None, A.min))
+    v.wait_ge(S.gs, 3)
+    V(v.tensor_scalar(T.ngt[:, :], T.km[:, :], 0.0, -1.0, A.is_gt, A.mult))
+    v.wait_ge(S.gs, 5)
+    V(v.tensor_copy(T.iqh[:, :], T.iq[:, :]))
+    V(v.tensor_copy(T.iuh[:, :], T.iu[:, :]))
+
+    v.wait_ge(S.il, 16)
+    V(v.tensor_scalar(T.own[:, :], T.idxk[:, :], 11, None, A.arith_shift_right))
+    V(v.tensor_scalar(T.loci[:, :], T.idxk[:, :], RC - 1, None, A.bitwise_and))
+    vw()
+    for i in range(NS):
+        V(v.tensor_scalar(T.oh[:, 8 * i:8 * i + 8], T.own[:, :], float((me + 1 + i) % NR), None, A.is_equal))
+    n_oh = c["v"]
+    V(v.tensor_copy(T.locf[:, :], T.loci[:, :]))
+    vw()
+    V(v.tensor_tensor_scan(T.ch[:, :], T.zm[:, :], T.oh[:, :], 0.0, A.mult, A.add))
+    n_ch = c["v"]
+    pe.wait_ge(S.vs, n_oh)
+    pe.matmul(T.sp[:, 0:64], T.ngt[:, :], T.oh[:, :], False, False)
+    pe.wait_ge(S.vs, n_ch)
+    PEI(pe.matmul(T.sp[:, 0:64], T.ones[:, :], T.ch[:, :], False, True))
+    v.wait_ge(S.ps, c["p"])
+    V(v.tensor_tensor(T.t1[:, :], T.sp[:, 0:64], T.oh[:, :], A.mult))
+    vw()
+    V(v.tensor_tensor(T.t32[:, :], T.t1[:, 0:32], T.t1[:, 32:64], A.add))
+    vw()
+    V(v.tensor_tensor(T.t16[:, :], T.t32[:, 0:16], T.t32[:, 16:32], A.add))
+    vw()
+    V(v.tensor_tensor(T.pos1[:, :], T.t16[:, 0:8], T.t16[:, 8:16], A.add))
+    vw()
+    V(v.tensor_scalar(T.u1[:, :], T.pos1[:, :], 7.5, 134217728.0, A.add, A.add))
+    vw()
+    V(v.tensor_scalar(T.u16[:, :], T.u1[:, :], 134217744.0, None, A.subtract))
+    vw()
+    for k in range(8):
+        a = T.am[:, 128 * k:128 * (k + 1)]
+        b = T.bm[:, 128 * k:128 * (k + 1)]
+        V(v.tensor_scalar(a, T.iqh[:, :], T.u16[:, k:k + 1], T.pos1[:, k:k + 1], A.add, A.is_equal))
+        V(v.tensor_scalar(b, T.iuh[:, :], T.u16[:, k:k + 1], T.locf[:, k:k + 1], A.is_equal, A.mult))
+        pe.wait_ge(S.vs, c["v"])
+        ins = pe.matmul(T.rqp[:, 0:128], a, b, k == 0, k == 7)
+    PEI(ins)
+    v.wait_ge(S.ps, c["p"])
+    v.tensor_copy(T.reqw[:, :], T.rqp[:, 0:128]).then_inc(S.rdy, 1)
+
+    Hc = P["H"][me]
+    up = _upmask(topo, P, me)
+    half = RC // 2
+    g.wait_ge(S.tl0, 16)
+    g.wait_ge(S.tl1, 16)
+    tsent = _send(g, core, T, topo, Hc, T.big[:, LAND:LAND + half], T.big[:, LAND:LAND + half], S.tarr, S.tsent, up)
+    g.wait_ge(S.rdy, 1)
+    sent = 0
+    order = P["reqorder"][me]
+    for lo in range(0, NS, 4):
+        trs = []
+        for i, o in enumerate(order[lo:lo + 4]):
+            dst = P["relay"].get((me, o), P["server"][(me, o)][0])
+            rid, pid = topo.addr(dst, core)
+            eng = _bits(topo.mask(core, dst))
+            s = _slot(me, o)
+            trs.append(RemoteDMATransfer(dst_ids=[DstId(rid=rid, pnc=pid)], dma_engine_mask=(1 << eng[2 * i]) | (1 << eng[2 * i + 1]),
+                                         remote_sem=S["rq%d" % me], src=T.reqw[:, 16 * s:16 * (s + 1)], dst=T["rq%d" % me][:, :]))
+            sent += 2
+        g.remote_dma_fused(trs, local_sem=S.sent)
+    g.wait_ge(S.tl2, 16)
+    g.wait_ge(S.tl3, 16)
+    tsent += _send(g, core, T, topo, Hc, T.big[:, LAND + half:LAND + RC], T.big[:, LAND + half:LAND + RC], S.tarr, S.tsent, up)
+    sy.wait_ge(S.tsent, tsent)
+    sy.dma_start(T.xs[:, :], T.x[:, :]).then_inc(S.xl, 16)
+
+    v.wait_ge(S.gs, 7)
+    V(v.tensor_scalar(T.rp2[:, :], T.rp[:, :], 3, None, A.arith_shift_right))
+    V(v.tensor_scalar(T.bm2i[:, :], T.bmi[:, :], 7, None, A.bitwise_and))
+    V(v.tensor_scalar(T.ohme[:, :], T.own[:, :], float(me), None, A.is_equal))
+    V(v.tensor_scalar(T.l2[:, :], T.locf[:, :], float(LAND + 1), None, A.add))
+    vw()
+    V(v.tensor_scalar(T.rep2[:, :], T.rp2[:, :], 0.0, None, A.is_equal))
+    V(v.tensor_scalar(T.bm2[:, :], T.bm2i[:, :], 0.0, None, A.is_equal))
+    V(v.tensor_tensor(T.l3[:, :], T.l2[:, :], T.ohme[:, :], A.mult))
+    vw()
+    V(v.tensor_tensor(T.pf[:, :], T.l3[:, :], T.pos1[:, :], A.add))
+    vw()
+    for k in range(8):
+        V(v.tensor_scalar(T.rbig[:, 8 * k:8 * k + 8], T.pf[:, :], T.bm2[:, k:k + 1], None, A.mult))
+    pe.wait_ge(S.vs, c["v"])
+    PEI(pe.matmul(T.pwp[:, 0:64], T.rep2[:, :], T.rbig[:, :], True, True))
+    v.wait_ge(S.ps, c["p"])
+    V(v.tensor_scalar(T.posw[:, :], T.pwp[:, 0:64], -1.0, None, A.add))
+
+    def tabwait(e):
+        for i in range(4):
+            e.wait_ge(S["tl%d" % i], 16)
+    sent += _serve(g, core, T, topo, P, tabwait)
+
+    narr = 0
+    for o in range(NR):
+        if o != me:
+            last = P["relay"].get((me, o), P["server"][(me, o)][0])
+            narr += len(_bits(topo.mask(last, core)))
+    vw()
+    v.wait_ge(S.xl, 16)
+    v.wait_ge(S.arr, narr)
+    for i in range(4):
+        blk = T.xs[:, 256 * i:256 * (i + 1)]
+        v.tensor_tensor(blk, T.big[:, 0:LAND + RC].indirect(T.posw[:, 16 * i:16 * (i + 1)]), blk, A.add).then_inc(S["fin%d" % i], 1)
+        q = sy if i % 2 == 0 else sc
+        q.wait_ge(S["fin%d" % i], 1)
+        q.dma_start(T.y[:, 256 * i:256 * (i + 1)], blk).then_inc(S.st, 16)
+    g.wait_ge(S.st, 64)
+    g.wait_ge(S.sent, sent)
+    g.wait_ge(S.vs, c["v"])
+    g.wait_ge(S.ps, c["p"])
+    g.wait_ge(S.gs, c["g"])
+
+
+def rank_program(g, core, T, topo):
+    P = _plan(T, topo)
+    if T.rank_of(core) is not None:
+        _rank(g, core, T, topo, P)
+    elif core in P["H"]:
+        _helper(g, core, T, topo, P, P["H"].index(core))
+    elif core in P["rel_of"]:
+        _relay(g, core, T, topo, P)

@@ -6,6 +6,7 @@ RC = 2048
 CAP = 256
 NS = NR - 1
 LAND = NS * CAP
+TB = [0, 256, 1024, 1536, 2048]
 
 SCRATCH = {
     "big": ("sbuf", [128, LAND + RC], "float32"),
@@ -55,7 +56,7 @@ SCRATCH = {
 for _r in range(NR):
     SCRATCH["rq%d" % _r] = ("sbuf", [128, 16], "uint16")
 
-SEMAPHORES = (["il", "tl0", "tl1", "tl2", "tl3", "xl", "vs", "ps", "gs", "rdy", "tarr", "tsent", "sent", "arr", "rsp",
+SEMAPHORES = (["il", "tl0", "tl1", "tl2", "tl3", "xl", "vs", "ps", "gs", "rdy", "tarr", "tsent", "sent", "arr", "rsp", "rsp2",
                "st", "gd0", "gd1", "gd2", "gd3", "fin0", "fin1", "fin2", "fin3"] + ["rq%d" % _r for _r in range(NR)])
 
 _PLAN = {}
@@ -96,7 +97,9 @@ def _plan(T, topo):
             order += [d0[i], d1[i]]
         for i, (_, r, o) in enumerate(sorted(prs)):
             relay[(r, o)] = order[i]
-    server, jobs = {}, {}
+    dpart = {a: sorted(b for b in range(n) if (a, b) in relay) for a in range(n)}
+    turn = lambda r, o: (dpart[r].index(o) + dpart[o].index(r)) % len(dpart[r])
+    onR = {}
     for o in range(n):
         rs = sorted([r for r in range(n) if r != o], key=lambda r: (r - o) % n)
         nxt = {r: relay.get((r, o), R[r]) for r in rs}
@@ -110,10 +113,71 @@ def _plan(T, topo):
             key = (max(ca, sum(cab.values()) - ca), -sum(1 for r in a if (r, o) in relay), m)
             if best is None or key < best[0]:
                 best = (key, a)
-        a = best[1]
-        b = [r for r in rs if r not in a]
+        for r in rs:
+            onR[(r, o)] = r in best[1]
+    cable = {}
+    for cs in bychip.values():
+        for d in set(topo.die(c) for c in cs):
+            for i, c in enumerate([c for c in cs if topo.die(c) == d]):
+                cable[c] = (d, i // 2)
+
+    def links(s, d, first):
+        a, b, di = place(s), place(d), topo.die(s)
+        if rackof(s) == rackof(d):
+            return [("o", a, di), ("i", b, di)]
+        if topo.chip(s) == topo.chip(d):
+            return [("c", a, cable[s])]
+        if first:
+            return [("c", a, cable[s]), ("o", (topo.host(d), topo.chip(s)), di), ("i", b, di)]
+        mid = (topo.host(s), topo.chip(d))
+        return [("o", a, di), ("i", mid, di), ("c", mid, cable[s])]
+
+    def load():
+        tot = 0
+        for first in (True, False):
+            cnt = {}
+            for (r, o), f in onR.items():
+                s = R[o] if f else H[o]
+                hops = [(s, relay[(r, o)]), (relay[(r, o)], R[r])] if (r, o) in relay else [(s, R[r])]
+                for x, y in hops:
+                    for l in links(x, y, first):
+                        cnt[l] = cnt.get(l, 0) + 1
+            tot += sum((3 if l[0] == "c" else 1) * k ** 3 for l, k in cnt.items())
+        return tot
+    cur, moved = load(), True
+    while moved:
+        moved = False
+        for o in range(n):
+            rs = [r for r in range(n) if r != o and (r, o) not in relay]
+            for a in rs:
+                for b in rs:
+                    if onR[(a, o)] and not onR[(b, o)]:
+                        onR[(a, o)], onR[(b, o)] = False, True
+                        t = load()
+                        if t < cur:
+                            cur, moved = t, True
+                        else:
+                            onR[(a, o)], onR[(b, o)] = True, False
+        for pr in sorted(relay):
+            for c in bychip[place(relay[pr])]:
+                if c in relay.values():
+                    continue
+                old = relay[pr]
+                relay[pr] = c
+                t = load()
+                if t < cur:
+                    cur, moved = t, True
+                else:
+                    relay[pr] = old
+    server, jobs, split = {}, {}, set()
+    for o in range(n):
+        rs = sorted([r for r in range(n) if r != o], key=lambda r: (r - o) % n)
+        a = [r for r in rs if onR[(r, o)]]
+        b = [r for r in rs if not onR[(r, o)]]
         for srv, mine, lead in ((R[o], a, 1), (H[o], b, 0)):
-            dg = [r for r in mine if (r, o) in relay]
+            dg = sorted([r for r in mine if (r, o) in relay], key=lambda r: turn(r, o))
+            if dg:
+                split.add((dg[-1], o))
             di = [r for r in mine if (r, o) not in relay]
             order = di[:lead] + dg + di[lead:]
             jobs[srv] = [(r, o) for r in order]
@@ -121,13 +185,23 @@ def _plan(T, topo):
                 server[(r, o)] = (srv, i)
     reqorder = {}
     for r in range(n):
-        reqorder[r] = sorted([o for o in range(n) if o != r], key=lambda o: (0 if (r, o) in relay else 1, server[(r, o)][1], (o - r) % n))
+        reqorder[r] = sorted([o for o in range(n) if o != r],
+                             key=lambda o: (0, turn(r, o), 0) if (r, o) in relay else (1, server[(r, o)][1], (o - r) % n))
     rel_of = {}
     for pr, c in relay.items():
         rel_of[c] = pr
-    p = {"R": R, "H": H, "relay": relay, "server": server, "jobs": jobs, "reqorder": reqorder, "rel_of": rel_of}
+    p = {"R": R, "H": H, "relay": relay, "server": server, "jobs": jobs, "reqorder": reqorder, "rel_of": rel_of, "split": split}
     _PLAN["p"] = p
     return p
+
+
+def _wide(k):
+    return k < 3 or k == NS - 1
+
+
+def _leng(topo, P, r, o):
+    dst = P["relay"].get((r, o), P["server"][(r, o)][0])
+    return len(_bits(topo.mask(P["R"][r], dst))) if _wide(P["reqorder"][r].index(o)) else 2
 
 
 def _slot(r, o):
@@ -147,7 +221,7 @@ def _serve(g, core, T, topo, P, tabwait):
         e = g.vector if i % 2 == 0 else g.scalar
         if i < 2:
             tabwait(e)
-        inc = len(_bits(topo.mask(P["relay"][(r, o)], core))) if (r, o) in P["relay"] else 2
+        inc = len(_bits(topo.mask(P["relay"][(r, o)], core))) if (r, o) in P["relay"] else _leng(topo, P, r, o)
         e.wait_ge(T.sem["rq%d" % r], inc)
         src = T.big[:, LAND:LAND + RC].indirect(T["rq%d" % r][:, :])
         out = T.resp[:, CAP * i:CAP * (i + 1)]
@@ -160,7 +234,12 @@ def _serve(g, core, T, topo, P, tabwait):
     for i, (r, o) in enumerate(jobs):
         g.wait_ge(T.sem["gd%d" % i], 1)
         src = T.resp[:, CAP * i:CAP * (i + 1)]
-        if (r, o) in P["relay"]:
+        if (r, o) in P["split"]:
+            hf = CAP // 2
+            rl = P["relay"][(r, o)]
+            sent += _send(g, core, T, topo, rl, T.big[:, 0:hf], T.resp[:, CAP * i:CAP * i + hf], T.sem.rsp, T.sem.sent)
+            sent += _send(g, core, T, topo, rl, T.big[:, hf:CAP], T.resp[:, CAP * i + hf:CAP * (i + 1)], T.sem.rsp2, T.sem.sent)
+        elif (r, o) in P["relay"]:
             sent += _send(g, core, T, topo, P["relay"][(r, o)], T.big[:, 0:CAP], src, T.sem.rsp, T.sem.sent)
         else:
             s = _slot(r, o)
@@ -172,26 +251,29 @@ def _relay(g, core, T, topo, P):
     r, o = P["rel_of"][core]
     srv = P["server"][(r, o)][0]
     buf = T["rq%d" % r]
-    g.wait_ge(T.sem["rq%d" % r], 2)
+    g.wait_ge(T.sem["rq%d" % r], _leng(topo, P, r, o))
     sent = _send(g, core, T, topo, srv, buf[:, :], buf[:, :], T.sem["rq%d" % r], T.sem.sent)
-    g.wait_ge(T.sem.rsp, len(_bits(topo.mask(srv, core))))
     s = _slot(r, o)
-    sent += _send(g, core, T, topo, P["R"][r], T.big[:, CAP * s:CAP * (s + 1)], T.big[:, 0:CAP], T.sem.arr, T.sem.sent)
+    cuts = [0, CAP // 2, CAP] if (r, o) in P["split"] else [0, CAP]
+    for k in range(len(cuts) - 1):
+        g.wait_ge(T.sem["rsp" if k == 0 else "rsp2"], len(_bits(topo.mask(srv, core))))
+        sent += _send(g, core, T, topo, P["R"][r], T.big[:, CAP * s + cuts[k]:CAP * s + cuts[k + 1]], T.big[:, cuts[k]:cuts[k + 1]],
+                      T.sem.arr, T.sem.sent)
     g.wait_ge(T.sem.sent, sent)
 
 
 def _helper(g, core, T, topo, P, owner):
-    up = len(_bits(_upmask(topo, P, owner)))
+    total = 2 * len(_bits(_upmask(topo, P, owner))) + len(_bits(topo.mask(P["R"][owner], core)))
 
     def tabwait(e):
-        e.wait_ge(T.sem.tarr, 2 * up)
+        e.wait_ge(T.sem.tarr, total)
     sent = _serve(g, core, T, topo, P, tabwait)
     g.wait_ge(T.sem.sent, sent)
 
 
 def _upmask(topo, P, o):
-    other = P["R"][(o + 1) % NR]
-    return topo.mask(P["R"][o], P["H"][o]) & ~topo.mask(P["R"][o], other)
+    off = [c for c in P["R"] if c != P["R"][o] and topo.may_write(P["R"][o], c)][0]
+    return topo.mask(P["R"][o], P["H"][o]) & ~topo.mask(P["R"][o], off)
 
 
 def _rank(g, core, T, topo, P):
@@ -218,16 +300,14 @@ def _rank(g, core, T, topo, P):
 
     sy.dma_start(T.idxk[:, :], T.idx[:, :]).then_inc(S.il, 16)
     for i in range(4):
-        q = sy if i % 2 == 0 else sc
-        q.dma_start(T.big[:, LAND + 512 * i:LAND + 512 * (i + 1)], T.tab[:, 512 * i:512 * (i + 1)]).then_inc(S["tl%d" % i], 16)
+        q = sc if i % 2 == 0 else sy
+        q.dma_start(T.big[:, LAND + TB[i]:LAND + TB[i + 1]], T.tab[:, TB[i]:TB[i + 1]]).then_inc(S["tl%d" % i], 16)
 
     G(g.iota(T.c3[:, :], [[2, 8], [0, 8]], 0, 0, allow_small_or_imprecise_dtypes=True))
     G(g.iota(T.zc[:, :], [[0, 8], [1, 8]], 0, 0, allow_small_or_imprecise_dtypes=True))
     G(g.iota(T.km[:, :], [[-1, 128]], 0, 1, allow_small_or_imprecise_dtypes=True))
     G(g.iota(T.iq[:, :], [[0, 8], [1, 16]], 1, 0, allow_small_or_imprecise_dtypes=True))
     G(g.iota(T.iu[:, :], [[16, 128]], 0, 0, allow_small_or_imprecise_dtypes=True))
-    G(g.iota(T.rp[:, :], [[0, 8], [-8, 16]], 0, 1))
-    G(g.iota(T.bmi[:, :], [[-1, 8]], 8, 1))
     V(v.memset(T.ones[:, :], 1.0))
     pe.wait_ge(S.gs, 1)
     pe.wait_ge(S.vs, 1)
@@ -281,27 +361,36 @@ def _rank(g, core, T, topo, P):
 
     Hc = P["H"][me]
     up = _upmask(topo, P, me)
-    half = RC // 2
+
+    def copy(lo, hi, m):
+        return _send(g, core, T, topo, Hc, T.big[:, LAND + lo:LAND + hi], T.big[:, LAND + lo:LAND + hi], S.tarr, S.tsent, m)
     g.wait_ge(S.tl0, 16)
+    tsent = copy(TB[0], TB[1], up)
     g.wait_ge(S.tl1, 16)
-    tsent = _send(g, core, T, topo, Hc, T.big[:, LAND:LAND + half], T.big[:, LAND:LAND + half], S.tarr, S.tsent, up)
+    tsent += copy(TB[1], TB[2], up)
     g.wait_ge(S.rdy, 1)
     sent = 0
     order = P["reqorder"][me]
-    for lo in range(0, NS, 4):
-        trs = []
-        for i, o in enumerate(order[lo:lo + 4]):
-            dst = P["relay"].get((me, o), P["server"][(me, o)][0])
-            rid, pid = topo.addr(dst, core)
-            eng = _bits(topo.mask(core, dst))
-            s = _slot(me, o)
-            trs.append(RemoteDMATransfer(dst_ids=[DstId(rid=rid, pnc=pid)], dma_engine_mask=(1 << eng[2 * i]) | (1 << eng[2 * i + 1]),
-                                         remote_sem=S["rq%d" % me], src=T.reqw[:, 16 * s:16 * (s + 1)], dst=T["rq%d" % me][:, :]))
-            sent += 2
-        g.remote_dma_fused(trs, local_sem=S.sent)
+    trs = []
+    for k, o in enumerate(order):
+        dst = P["relay"].get((me, o), P["server"][(me, o)][0])
+        s = _slot(me, o)
+        if _wide(k):
+            sent += _send(g, core, T, topo, dst, T["rq%d" % me][:, :], T.reqw[:, 16 * s:16 * (s + 1)], S["rq%d" % me], S.sent)
+            continue
+        rid, pid = topo.addr(dst, core)
+        eng = _bits(topo.mask(core, dst))
+        i = len(trs)
+        trs.append(RemoteDMATransfer(dst_ids=[DstId(rid=rid, pnc=pid)], dma_engine_mask=(1 << eng[2 * i]) | (1 << eng[2 * i + 1]),
+                                     remote_sem=S["rq%d" % me], src=T.reqw[:, 16 * s:16 * (s + 1)], dst=T["rq%d" % me][:, :]))
+        sent += 2
+        if len(trs) == 4:
+            g.remote_dma_fused(trs, local_sem=S.sent)
     g.wait_ge(S.tl2, 16)
     g.wait_ge(S.tl3, 16)
-    tsent += _send(g, core, T, topo, Hc, T.big[:, LAND + half:LAND + RC], T.big[:, LAND + half:LAND + RC], S.tarr, S.tsent, up)
+    tsent += copy(TB[2], TB[4], topo.mask(core, Hc))
+    G(g.iota(T.rp[:, :], [[0, 8], [-8, 16]], 0, 1))
+    G(g.iota(T.bmi[:, :], [[-1, 8]], 8, 1))
     sy.wait_ge(S.tsent, tsent)
     sy.dma_start(T.xs[:, :], T.x[:, :]).then_inc(S.xl, 16)
 
@@ -333,7 +422,7 @@ def _rank(g, core, T, topo, P):
     for o in range(NR):
         if o != me:
             last = P["relay"].get((me, o), P["server"][(me, o)][0])
-            narr += len(_bits(topo.mask(last, core)))
+            narr += len(_bits(topo.mask(last, core))) * (2 if (me, o) in P["split"] else 1)
     vw()
     v.wait_ge(S.xl, 16)
     v.wait_ge(S.arr, narr)

from concourse.bass import DstId, RemoteDMATransfer
from concourse.mybir import AluOpType, ActivationFunctionType

NR = 9
RC = 2048
CAP = 256
NS = NR - 1
LAND = NS * CAP
TB = [0, 256, 1024, 1536, 2048]

SCRATCH = {
    "big": ("sbuf", [128, LAND + RC], "float32"),
    "resp": ("sbuf", [128, 4 * CAP], "float32"),
    "xs": ("sbuf", [128, 1024], "float32"),
    "idxk": ("sbuf", [128, 8], "int32"),
    "own": ("sbuf", [128, 8], "int32"),
    "loci": ("sbuf", [128, 8], "int32"),
    "locf": ("sbuf", [128, 8], "float32"),
    "oh": ("sbuf", [128, 64], "bfloat16"),
    "ch": ("sbuf", [128, 64], "bfloat16"),
    "zc": ("sbuf", [128, 64], "float32"),
    "zm": ("sbuf", [128, 64], "bfloat16"),
    "c3": ("sbuf", [128, 64], "bfloat16"),
    "ones": ("sbuf", [128, 128], "bfloat16"),
    "km": ("sbuf", [128, 128], "float32"),
    "ngt": ("sbuf", [128, 128], "bfloat16"),
    "iq": ("sbuf", [128, 128], "float32"),
    "iu": ("sbuf", [128, 128], "float32"),
    "iqh": ("sbuf", [128, 128], "float16"),
    "iuh": ("sbuf", [128, 128], "float16"),
    "t1": ("sbuf", [128, 64], "float32"),
    "t32": ("sbuf", [128, 32], "float32"),
    "t16": ("sbuf", [128, 16], "float32"),
    "pos1": ("sbuf", [128, 8], "float32"),
    "u1": ("sbuf", [128, 8], "float32"),
    "u16": ("sbuf", [128, 8], "float32"),
    "am": ("sbuf", [128, 1024], "float16"),
    "bm": ("sbuf", [128, 1024], "float16"),
    "reqw": ("sbuf", [128, 128], "uint16"),
    "rp": ("sbuf", [128, 128], "int32"),
    "rp2": ("sbuf", [128, 128], "int32"),
    "rep2": ("sbuf", [128, 128], "float32"),
    "bmi": ("sbuf", [128, 8], "int32"),
    "bm2i": ("sbuf", [128, 8], "int32"),
    "bm2": ("sbuf", [128, 8], "float32"),
    "ohme": ("sbuf", [128, 8], "float32"),
    "l2": ("sbuf", [128, 8], "float32"),
    "l3": ("sbuf", [128, 8], "float32"),
    "pf": ("sbuf", [128, 8], "float32"),
    "rbig": ("sbuf", [128, 64], "float32"),
    "posw": ("sbuf", [128, 64], "uint16"),
    "sp": ("psum", [128, 512], "float32"),
    "rqp": ("psum", [128, 512], "float32"),
    "pwp": ("psum", [128, 512], "float32"),
}
for _r in range(NR):
    SCRATCH["rq%d" % _r] = ("sbuf", [128, 16], "uint16")

SEMAPHORES = (["il", "tl0", "tl1", "tl2", "tl3", "xl", "vs", "ps", "gs", "rdy", "tarr", "tsent", "sent", "arr", "rsp", "rsp2",
               "st", "gd0", "gd1", "gd2", "gd3", "fin0", "fin1", "fin2", "fin3"] + ["rq%d" % _r for _r in range(NR)])

_PLAN = {}


def _bits(mask):
    return [e for e in range(16) if (mask >> e) & 1]


def _plan(T, topo):
    if "p" in _PLAN:
        return _PLAN["p"]
    R = list(T.cores)
    n = len(R)
    allc = range(4 * topo.CORES_PER_HOST)
    place = lambda c: (topo.host(c), topo.chip(c))
    bychip = {}
    for c in allc:
        bychip.setdefault(place(c), []).append(c)
    rank_hosts = set(topo.host(c) for c in R)
    H = [[c for c in bychip[place(R[o])] if topo.die(c) != topo.die(R[o])][0] for o in range(n)]
    rackof = lambda c: topo.rack(topo.host(c))
    diag = [(r, o) for r in range(n) for o in range(n) if r != o and not topo.may_write(R[o], R[r])]
    groups = {}
    for (r, o) in diag:
        zs = [h for h in range(4) if h not in rank_hosts
              and topo.may_write(R[r], bychip[(h, topo.chip(R[r]))][0]) and topo.may_write(R[o], bychip[(h, topo.chip(R[o]))][0])]
        z = zs[0]
        far = r if rackof(R[r]) != topo.rack(z) else o
        groups.setdefault((z, topo.chip(R[far])), []).append((0 if far == r else 1, r, o))
    relay = {}
    for key, prs in groups.items():
        cs = bychip[key]
        d0 = [c for c in cs if topo.die(c) == topo.die(cs[0])]
        d1 = [c for c in cs if topo.die(c) != topo.die(cs[0])]
        order = []
        for i in list(range(0, len(d0), 2)) + list(range(1, len(d0), 2)):
            order += [d0[i], d1[i]]
        for i, (_, r, o) in enumerate(sorted(prs)):
            relay[(r, o)] = order[i]
    dpart = {a: sorted(b for b in range(n) if (a, b) in relay) for a in range(n)}
    turn = lambda r, o: (dpart[r].index(o) + dpart[o].index(r)) % len(dpart[r])
    onR = {}
    for o in range(n):
        rs = sorted([r for r in range(n) if r != o], key=lambda r: (r - o) % n)
        nxt = {r: relay.get((r, o), R[r]) for r in rs}
        cab = {r: rackof(nxt[r]) != rackof(R[o]) for r in rs}
        best = None
        for m in range(1 << len(rs)):
            a = [rs[i] for i in range(len(rs)) if (m >> i) & 1]
            if len(a) != len(rs) // 2:
                continue
            ca = sum(1 for r in a if cab[r])
            key = (max(ca, sum(cab.values()) - ca), -sum(1 for r in a if (r, o) in relay), m)
            if best is None or key < best[0]:
                best = (key, a)
        for r in rs:
            onR[(r, o)] = r in best[1]
    cable = {}
    for cs in bychip.values():
        for d in set(topo.die(c) for c in cs):
            for i, c in enumerate([c for c in cs if topo.die(c) == d]):
                cable[c] = (d, i // 2)

    def links(s, d, first):
        a, b, di = place(s), place(d), topo.die(s)
        if rackof(s) == rackof(d):
            return [("o", a, di), ("i", b, di)]
        if topo.chip(s) == topo.chip(d):
            return [("c", a, cable[s])]
        if first:
            return [("c", a, cable[s]), ("o", (topo.host(d), topo.chip(s)), di), ("i", b, di)]
        mid = (topo.host(s), topo.chip(d))
        return [("o", a, di), ("i", mid, di), ("c", mid, cable[s])]

    def load():
        tot = 0
        for first in (True, False):
            cnt = {}
            for (r, o), f in onR.items():
                s = R[o] if f else H[o]
                hops = [(s, relay[(r, o)]), (relay[(r, o)], R[r])] if (r, o) in relay else [(s, R[r])]
                for x, y in hops:
                    for l in links(x, y, first):
                        cnt[l] = cnt.get(l, 0) + 1
            tot += sum((3 if l[0] == "c" else 1) * k ** 3 for l, k in cnt.items())
        return tot
    cur, moved = load(), True
    while moved:
        moved = False
        for o in range(n):
            rs = [r for r in range(n) if r != o and (r, o) not in relay]
            for a in rs:
                for b in rs:
                    if onR[(a, o)] and not onR[(b, o)]:
                        onR[(a, o)], onR[(b, o)] = False, True
                        t = load()
                        if t < cur:
                            cur, moved = t, True
                        else:
                            onR[(a, o)], onR[(b, o)] = True, False
        for pr in sorted(relay):
            for c in bychip[place(relay[pr])]:
                if c in relay.values():
                    continue
                old = relay[pr]
                relay[pr] = c
                t = load()
                if t < cur:
                    cur, moved = t, True
                else:
                    relay[pr] = old
    server, jobs, split = {}, {}, set()
    for o in range(n):
        rs = sorted([r for r in range(n) if r != o], key=lambda r: (r - o) % n)
        a = [r for r in rs if onR[(r, o)]]
        b = [r for r in rs if not onR[(r, o)]]
        for srv, mine, lead in ((R[o], a, 1), (H[o], b, 0)):
            dg = sorted([r for r in mine if (r, o) in relay], key=lambda r: turn(r, o))
            if dg:
                split.add((dg[-1], o))
            di = [r for r in mine if (r, o) not in relay]
            order = di[:lead] + dg + di[lead:]
            jobs[srv] = [(r, o) for r in order]
            for i, r in enumerate(order):
                server[(r, o)] = (srv, i)
    reqorder = {}
    for r in range(n):
        reqorder[r] = sorted([o for o in range(n) if o != r],
                             key=lambda o: (0, turn(r, o), 0) if (r, o) in relay else (1, server[(r, o)][1], (o - r) % n))
    rel_of = {}
    for pr, c in relay.items():
        rel_of[c] = pr
    p = {"R": R, "H": H, "relay": relay, "server": server, "jobs": jobs, "reqorder": reqorder, "rel_of": rel_of, "split": split}
    _PLAN["p"] = p
    return p


def _wide(k):
    return k < 3 or k == NS - 1


def _leng(topo, P, r, o):
    dst = P["relay"].get((r, o), P["server"][(r, o)][0])
    return len(_bits(topo.mask(P["R"][r], dst))) if _wide(P["reqorder"][r].index(o)) else 2


def _slot(r, o):
    return (o - r - 1) % NR


def _send(g, core, T, topo, dst, out_ap, in_ap, rsem, lsem, mask=None):
    rid, pid = topo.addr(dst, core)
    m = topo.mask(core, dst) if mask is None else mask
    g.remote_dma(out_ap, in_ap, rsem, lsem, pid, rid, m)
    return len(_bits(m))


def _serve(g, core, T, topo, P, tabwait):
    jobs = P["jobs"][core]
    for i, (r, o) in enumerate(jobs):
        e = g.vector if i % 2 == 0 else g.scalar
        if i < 2:
            tabwait(e)
        inc = len(_bits(topo.mask(P["relay"][(r, o)], core))) if (r, o) in P["relay"] else _leng(topo, P, r, o)
        e.wait_ge(T.sem["rq%d" % r], inc)
        src = T.big[:, LAND:LAND + RC].indirect(T["rq%d" % r][:, :])
        out = T.resp[:, CAP * i:CAP * (i + 1)]
        if i % 2 == 0:
            ins = g.vector.tensor_copy(out, src)
        else:
            ins = g.scalar.activation(out, src, ActivationFunctionType.Copy)
        ins.then_inc(T.sem["gd%d" % i], 1)
    sent = 0
    for i, (r, o) in enumerate(jobs):
        g.wait_ge(T.sem["gd%d" % i], 1)
        src = T.resp[:, CAP * i:CAP * (i + 1)]
        if (r, o) in P["split"]:
            hf = CAP // 2
            rl = P["relay"][(r, o)]
            sent += _send(g, core, T, topo, rl, T.big[:, 0:hf], T.resp[:, CAP * i:CAP * i + hf], T.sem.rsp, T.sem.sent)
            sent += _send(g, core, T, topo, rl, T.big[:, hf:CAP], T.resp[:, CAP * i + hf:CAP * (i + 1)], T.sem.rsp2, T.sem.sent)
        elif (r, o) in P["relay"]:
            sent += _send(g, core, T, topo, P["relay"][(r, o)], T.big[:, 0:CAP], src, T.sem.rsp, T.sem.sent)
        else:
            s = _slot(r, o)
            sent += _send(g, core, T, topo, P["R"][r], T.big[:, CAP * s:CAP * (s + 1)], src, T.sem.arr, T.sem.sent)
    return sent


def _relay(g, core, T, topo, P):
    r, o = P["rel_of"][core]
    srv = P["server"][(r, o)][0]
    buf = T["rq%d" % r]
    g.wait_ge(T.sem["rq%d" % r], _leng(topo, P, r, o))
    sent = _send(g, core, T, topo, srv, buf[:, :], buf[:, :], T.sem["rq%d" % r], T.sem.sent)
    s = _slot(r, o)
    cuts = [0, CAP // 2, CAP] if (r, o) in P["split"] else [0, CAP]
    for k in range(len(cuts) - 1):
        g.wait_ge(T.sem["rsp" if k == 0 else "rsp2"], len(_bits(topo.mask(srv, core))))
        sent += _send(g, core, T, topo, P["R"][r], T.big[:, CAP * s + cuts[k]:CAP * s + cuts[k + 1]], T.big[:, cuts[k]:cuts[k + 1]],
                      T.sem.arr, T.sem.sent)
    g.wait_ge(T.sem.sent, sent)


def _helper(g, core, T, topo, P, owner):
    total = 2 * len(_bits(_upmask(topo, P, owner))) + len(_bits(topo.mask(P["R"][owner], core)))

    def tabwait(e):
        e.wait_ge(T.sem.tarr, total)
    sent = _serve(g, core, T, topo, P, tabwait)
    g.wait_ge(T.sem.sent, sent)


def _upmask(topo, P, o):
    off = [c for c in P["R"] if c != P["R"][o] and topo.may_write(P["R"][o], c)][0]
    return topo.mask(P["R"][o], P["H"][o]) & ~topo.mask(P["R"][o], off)


def _rank(g, core, T, topo, P):
    A = AluOpType
    v, pe, sc, sy = g.vector, g.tensor, g.scalar, g.sync
    S = T.sem
    me = T.rank_of(core)
    c = {"v": 0, "p": 0, "g": 0}

    def V(ins):
        ins.then_inc(S.vs, 1)
        c["v"] += 1

    def vw():
        v.wait_ge(S.vs, c["v"])

    def G(ins):
        ins.then_inc(S.gs, 1)
        c["g"] += 1

    def PEI(ins):
        ins.then_inc(S.ps, 1)
        c["p"] += 1

    sy.dma_start(T.idxk[:, :], T.idx[:, :]).then_inc(S.il, 16)
    for i in range(4):
        q = sc if i % 2 == 0 else sy
        q.dma_start(T.big[:, LAND + TB[i]:LAND + TB[i + 1]], T.tab[:, TB[i]:TB[i + 1]]).then_inc(S["tl%d" % i], 16)

    G(g.iota(T.c3[:, :], [[2, 8], [0, 8]], 0, 0, allow_small_or_imprecise_dtypes=True))
    G(g.iota(T.zc[:, :], [[0, 8], [1, 8]], 0, 0, allow_small_or_imprecise_dtypes=True))
    G(g.iota(T.km[:, :], [[-1, 128]], 0, 1, allow_small_or_imprecise_dtypes=True))
    G(g.iota(T.iq[:, :], [[0, 8], [1, 16]], 1, 0, allow_small_or_imprecise_dtypes=True))
    G(g.iota(T.iu[:, :], [[16, 128]], 0, 0, allow_small_or_imprecise_dtypes=True))
    V(v.memset(T.ones[:, :], 1.0))
    pe.wait_ge(S.gs, 1)
    pe.wait_ge(S.vs, 1)
    pe.matmul(T.sp[:, 0:64], T.ones[:, :], T.c3[:, :], True, False)
    v.wait_ge(S.gs, 2)
    V(v.tensor_scalar(T.zm[:, :], T.zc[:, :], 1.0, None, A.min))
    v.wait_ge(S.gs, 3)
    V(v.tensor_scalar(T.ngt[:, :], T.km[:, :], 0.0, -1.0, A.is_gt, A.mult))
    v.wait_ge(S.gs, 5)
    V(v.tensor_copy(T.iqh[:, :], T.iq[:, :]))
    V(v.tensor_copy(T.iuh[:, :], T.iu[:, :]))

    v.wait_ge(S.il, 16)
    V(v.tensor_scalar(T.own[:, :], T.idxk[:, :], 11, None, A.arith_shift_right))
    V(v.tensor_scalar(T.loci[:, :], T.idxk[:, :], RC - 1, None, A.bitwise_and))
    vw()
    for i in range(NS):
        V(v.tensor_scalar(T.oh[:, 8 * i:8 * i + 8], T.own[:, :], float((me + 1 + i) % NR), None, A.is_equal))
    n_oh = c["v"]
    V(v.tensor_copy(T.locf[:, :], T.loci[:, :]))
    vw()
    V(v.tensor_tensor_scan(T.ch[:, :], T.zm[:, :], T.oh[:, :], 0.0, A.mult, A.add))
    n_ch = c["v"]
    pe.wait_ge(S.vs, n_oh)
    pe.matmul(T.sp[:, 0:64], T.ngt[:, :], T.oh[:, :], False, False)
    pe.wait_ge(S.vs, n_ch)
    PEI(pe.matmul(T.sp[:, 0:64], T.ones[:, :], T.ch[:, :], False, True))
    v.wait_ge(S.ps, c["p"])
    V(v.tensor_tensor(T.t1[:, :], T.sp[:, 0:64], T.oh[:, :], A.mult))
    vw()
    V(v.tensor_tensor(T.t32[:, :], T.t1[:, 0:32], T.t1[:, 32:64], A.add))
    vw()
    V(v.tensor_tensor(T.t16[:, :], T.t32[:, 0:16], T.t32[:, 16:32], A.add))
    vw()
    V(v.tensor_tensor(T.pos1[:, :], T.t16[:, 0:8], T.t16[:, 8:16], A.add))
    vw()
    V(v.tensor_scalar(T.u1[:, :], T.pos1[:, :], 7.5, 134217728.0, A.add, A.add))
    vw()
    V(v.tensor_scalar(T.u16[:, :], T.u1[:, :], 134217744.0, None, A.subtract))
    vw()
    for k in range(8):
        a = T.am[:, 128 * k:128 * (k + 1)]
        b = T.bm[:, 128 * k:128 * (k + 1)]
        V(v.tensor_scalar(a, T.iqh[:, :], T.u16[:, k:k + 1], T.pos1[:, k:k + 1], A.add, A.is_equal))
        V(v.tensor_scalar(b, T.iuh[:, :], T.u16[:, k:k + 1], T.locf[:, k:k + 1], A.is_equal, A.mult))
        pe.wait_ge(S.vs, c["v"])
        ins = pe.matmul(T.rqp[:, 0:128], a, b, k == 0, k == 7)
    PEI(ins)
    v.wait_ge(S.ps, c["p"])
    v.tensor_copy(T.reqw[:, :], T.rqp[:, 0:128]).then_inc(S.rdy, 1)

    Hc = P["H"][me]
    up = _upmask(topo, P, me)

    def copy(lo, hi, m):
        return _send(g, core, T, topo, Hc, T.big[:, LAND + lo:LAND + hi], T.big[:, LAND + lo:LAND + hi], S.tarr, S.tsent, m)
    g.wait_ge(S.tl0, 16)
    tsent = copy(TB[0], TB[1], up)
    g.wait_ge(S.tl1, 16)
    tsent += copy(TB[1], TB[2], up)
    g.wait_ge(S.rdy, 1)
    sent = 0
    order = P["reqorder"][me]
    trs = []
    for k, o in enumerate(order):
        dst = P["relay"].get((me, o), P["server"][(me, o)][0])
        s = _slot(me, o)
        if _wide(k):
            sent += _send(g, core, T, topo, dst, T["rq%d" % me][:, :], T.reqw[:, 16 * s:16 * (s + 1)], S["rq%d" % me], S.sent)
            continue
        rid, pid = topo.addr(dst, core)
        eng = _bits(topo.mask(core, dst))
        i = len(trs)
        trs.append(RemoteDMATransfer(dst_ids=[DstId(rid=rid, pnc=pid)], dma_engine_mask=(1 << eng[2 * i]) | (1 << eng[2 * i + 1]),
                                     remote_sem=S["rq%d" % me], src=T.reqw[:, 16 * s:16 * (s + 1)], dst=T["rq%d" % me][:, :]))
        sent += 2
        if len(trs) == 4:
            g.remote_dma_fused(trs, local_sem=S.sent)
    g.wait_ge(S.tl2, 16)
    g.wait_ge(S.tl3, 16)
    tsent += copy(TB[2], TB[4], topo.mask(core, Hc))
    G(g.iota(T.rp[:, :], [[0, 8], [-8, 16]], 0, 1))
    G(g.iota(T.bmi[:, :], [[-1, 8]], 8, 1))
    sy.wait_ge(S.tsent, tsent)
    sy.dma_start(T.xs[:, :], T.x[:, :]).then_inc(S.xl, 16)

    v.wait_ge(S.gs, 7)
    V(v.tensor_scalar(T.rp2[:, :], T.rp[:, :], 3, None, A.arith_shift_right))
    V(v.tensor_scalar(T.bm2i[:, :], T.bmi[:, :], 7, None, A.bitwise_and))
    V(v.tensor_scalar(T.ohme[:, :], T.own[:, :], float(me), None, A.is_equal))
    V(v.tensor_scalar(T.l2[:, :], T.locf[:, :], float(LAND + 1), None, A.add))
    vw()
    V(v.tensor_scalar(T.rep2[:, :], T.rp2[:, :], 0.0, None, A.is_equal))
    V(v.tensor_scalar(T.bm2[:, :], T.bm2i[:, :], 0.0, None, A.is_equal))
    V(v.tensor_tensor(T.l3[:, :], T.l2[:, :], T.ohme[:, :], A.mult))
    vw()
    V(v.tensor_tensor(T.pf[:, :], T.l3[:, :], T.pos1[:, :], A.add))
    vw()
    for k in range(8):
        V(v.tensor_scalar(T.rbig[:, 8 * k:8 * k + 8], T.pf[:, :], T.bm2[:, k:k + 1], None, A.mult))
    pe.wait_ge(S.vs, c["v"])
    PEI(pe.matmul(T.pwp[:, 0:64], T.rep2[:, :], T.rbig[:, :], True, True))
    v.wait_ge(S.ps, c["p"])
    V(v.tensor_scalar(T.posw[:, :], T.pwp[:, 0:64], -1.0, None, A.add))

    def tabwait(e):
        for i in range(4):
            e.wait_ge(S["tl%d" % i], 16)
    sent += _serve(g, core, T, topo, P, tabwait)

    narr = 0
    for o in range(NR):
        if o != me:
            last = P["relay"].get((me, o), P["server"][(me, o)][0])
            narr += len(_bits(topo.mask(last, core))) * (2 if (me, o) in P["split"] else 1)
    vw()
    v.wait_ge(S.xl, 16)
    v.wait_ge(S.arr, narr)
    for i in range(4):
        blk = T.xs[:, 256 * i:256 * (i + 1)]
        v.tensor_tensor(blk, T.big[:, 0:LAND + RC].indirect(T.posw[:, 16 * i:16 * (i + 1)]), blk, A.add).then_inc(S["fin%d" % i], 1)
        q = sy if i % 2 == 0 else sc
        q.wait_ge(S["fin%d" % i], 1)
        q.dma_start(T.y[:, 256 * i:256 * (i + 1)], blk).then_inc(S.st, 16)
    g.wait_ge(S.st, 64)
    g.wait_ge(S.sent, sent)
    g.wait_ge(S.vs, c["v"])
    g.wait_ge(S.ps, c["p"])
    g.wait_ge(S.gs, c["g"])


def rank_program(g, core, T, topo):
    P = _plan(T, topo)
    if T.rank_of(core) is not None:
        _rank(g, core, T, topo, P)
    elif core in P["H"]:
        _helper(g, core, T, topo, P, P["H"].index(core))
    elif core in P["rel_of"]:
        _relay(g, core, T, topo, P)
